import numpy as np
import ml_dtypes


def mxq(x, axis, fmt="e4m3"):
    dtype, down = {"e4m3": (ml_dtypes.float8_e4m3fn, 7), "e5m2": (ml_dtypes.float8_e5m2, 14)}[fmt]
    v = np.moveaxis(np.asarray(x, np.float32).astype(ml_dtypes.bfloat16).astype(np.float64), axis, -1)
    blocks = v.reshape(v.shape[:-1] + (-1, 32))
    amax = np.abs(blocks).max(-1, keepdims=True)
    byte = np.maximum(np.where(amax > 0, np.frexp(amax)[1] - 1 + 127, 0) - down, 1)
    scale = np.exp2(byte - 127.0)
    codes = (blocks / scale).astype(np.float32).astype(dtype).astype(np.float64)
    return np.moveaxis((codes * scale).reshape(v.shape), -1, axis)


WIDE = False


def mx_kscale(k):
    if not WIDE:
        return np.ones(k)
    levels = np.array([10, -10, 5, -5, 0])
    if k % 512:
        return np.exp2(np.random.permutation(np.resize(levels, k // 32))).repeat(32)
    a = np.empty((k // 512, 16))
    for p in range(k // 512):
        a[p, :8] = np.random.permutation(np.resize(levels, 8))
        for g in range(8):
            far = levels[np.abs(levels - a[p, g]) >= 10]
            a[p, g + 8] = far[np.random.randint(len(far))]
    return np.exp2(a.ravel()).repeat(32)


def f64(x):
    return np.asarray(x).astype(np.float64)


def striped(idx):
    return np.tile(idx.reshape(-1, 16).T, (8, 1)).astype(np.uint16)


def unstriped(offs):
    return offs[:16].T.reshape(-1).astype(np.int64)


E2M1 = np.array([0.0, 0.5, 1.0, 1.5, 2.0, 3.0, 4.0, 6.0, -0.0, -0.5, -1.0, -1.5, -2.0, -3.0, -4.0, -6.0])


def pack_weight(w, fmt):
    k, n = w.shape
    w = f64(np.asarray(w, np.float32).astype(ml_dtypes.bfloat16)).reshape(k // 32, 32, n)
    amax = np.abs(w).max(1)
    if fmt == "e4m3":
        byte = np.frexp(amax)[1] - 1 + 127 - 7
    else:
        mant, ex = np.frexp(amax / 6.0)
        byte = np.where(mant > 0.5, ex, ex - 1) + 127
    byte = np.clip(np.where(amax > 0, byte, 1), 1, 254)
    scaled = (w * np.exp2(127.0 - byte)[:, None, :]).reshape(k, n).astype(np.float32)
    by_word = np.ascontiguousarray(scaled.reshape(k // 512, 128, 4, n).transpose(0, 1, 3, 2))
    if fmt == "e4m3":
        words = by_word.astype(ml_dtypes.float8_e4m3fn).view(np.uint8)
    else:
        c = by_word.astype(ml_dtypes.float4_e2m1fn).view(np.uint8) & 0xF
        words = (c[..., 0::2] | (c[..., 1::2] << 4)).reshape(k // 512, 128, 2 * n)
    return np.ascontiguousarray(words), np.ascontiguousarray(byte.astype(np.uint8).reshape(k // 512, 16, n))


def unpack_weight(words, scales, fmt):
    g, _, n = scales.shape
    words = np.ascontiguousarray(words).reshape(g, 128, n, -1)
    if fmt == "e4m3":
        vals = words.view(ml_dtypes.float8_e4m3fn).astype(np.float64)
    else:
        nib = np.empty((g, 128, n, 4), np.uint8)
        nib[..., 0::2] = words & 0xF
        nib[..., 1::2] = words >> 4
        vals = E2M1[nib]
    vals = vals * np.repeat(np.exp2(scales.astype(np.float64) - 127.0), 8, axis=1)[..., None]
    return vals.transpose(0, 1, 3, 2).reshape(g * 512, n)


def relu(v):
    return np.maximum(v, 0.0)


K, T, E, C, N = 512, 640, 2, 256, 1024
M = 128


def by_expert(wq, xq):
    return np.concatenate([wq[e].T @ xq[:, e * C:(e + 1) * C] for e in range(E)], axis=1)


def setup_inputs():
    n = np.random.standard_normal
    s = mx_kscale(K)[:, None]
    v = mx_kscale(N)
    w = [pack_weight(m, "e2m1") for m in n((E, K, N)) / np.sqrt(K) / s[None] * v[None, None, :]]
    return {
        "xT": (n((K, T)) * s).astype(np.float32),
        "w_words": np.stack([m[0] for m in w]),
        "w_scales": np.stack([m[1] for m in w]),
        "b": (0.3 * n((N, E)) * v[:, None]).astype(np.float32),
        "wp": (n((N, M)) / np.sqrt(N) / v[:, None]).astype(np.float32),
        "gate": np.tile(np.random.uniform(0.2, 1.0, E * C), (N, 1)).astype(np.float32),
        "offs": striped(np.random.permutation(T)[:E * C]),
    }


def reference(xT, w_words, w_scales, b, wp, gate, offs):
    idx = unstriped(offs)
    w = np.stack([unpack_weight(w_words[e], w_scales[e], "e2m1") for e in range(E)])
    xq = mxq(f64(xT)[:, idx], 0, "e4m3")
    y = by_expert(w, xq)
    y = relu(y + np.repeat(f64(b), C, axis=1))
    c = np.zeros((N, T))
    c[:, idx] = f64(gate) * y
    return mxq(f64(wp), 0, "e4m3").T @ mxq(c, 0, "e4m3")

@@ -1,0 +1,181 @@
+from contextlib import ExitStack
+
+import concourse.mybir as mybir
+
+K, T, E, C, N, M = 512, 640, 2, 256, 1024, 128
+P = 128
+PACK = 4
+PASSES = N // 512
+
+FLOPS = 2 * E * C * K * N + 2 * E * C * N * M
+BYTES = 4 * K * T + E * K * N // 2 + E * K * N // 32 + 4 * N * E + 4 * N * M + 4 * E * C + 2 * P * (E * C // 16) + 4 * M * T
+
+F32 = mybir.dt.float32
+BF16 = mybir.dt.bfloat16
+I32 = mybir.dt.int32
+U32 = mybir.dt.uint32
+U16 = mybir.dt.uint16
+U8 = mybir.dt.uint8
+FP8X4 = mybir.dt.float8_e4m3fn_x4
+FP4X4 = mybir.dt.float4_e2m1fn_x4
+RELU = mybir.ActivationFunctionType.Relu
+MULT = mybir.AluOpType.mult
+
+
+def tile_moe_nxt_lin_relu_kernel(tc, xT, w_words, w_scales, b, wp, gate, offs, out):
+    nc = tc.nc
+    with ExitStack() as ctx:
+        keep = ctx.enter_context(tc.tile_pool(name="keep", bufs=1))
+        psum1 = ctx.enter_context(tc.psum_pool(name="psum1", bufs=6))
+        psum2 = ctx.enter_context(tc.psum_pool(name="psum2", bufs=2))
+
+        offsets = keep.tile([P, E * C // 16], U16, name="offsets")
+        w_raw = keep.tile([P, E, 2 * N], U8, align_bytes=64, name="w_raw")
+        w_perm = keep.tile([P, E, 2 * N], U8, align_bytes=64, name="w_perm")
+        s_raw = keep.tile([P, E, N], U8, align_bytes=64, name="s_raw")
+        s_perm = keep.tile([P, E, N], U8, align_bytes=64, name="s_perm")
+        codes = keep.tile([P, T], U32, align_bytes=64, name="codes")
+        scales = keep.tile([P, T], U8, align_bytes=64, name="scales")
+        bias = keep.tile([P, PASSES, PACK * E], F32, name="bias")
+        gates = keep.tile([P, E * C], F32, name="gates")
+        wp_raw = keep.tile([P, PASSES, PACK, M], F32, name="wp_raw")
+        wp_bf = keep.tile([P, PASSES, M, PACK], BF16, align_bytes=64, name="wp_bf")
+        wp_codes = keep.tile([P, PASSES * M], U32, align_bytes=64, name="wp_codes")
+        wp_scales = keep.tile([P, PASSES * M], U8, align_bytes=64, name="wp_scales")
+        result = keep.tile([P, T], F32, name="result")
+
+        nc.vector.memset(s_raw[:].rearrange("p e n -> p (e n)").bitcast(I32), 0)
+        nc.gpsimd.memset(scales[:], 0)
+        nc.gpsimd.memset(result[:], 0.0)
+
+        for e in range(E):
+            nc.sync.dma_start(out=w_raw[:, e, :].bitcast(I32), in_=w_words[e, 0].bitcast(I32))
+        for q in range(4):
+            nc.scalar.dma_start(
+                out=s_raw[32 * q : 32 * q + 4, :, :].bitcast(I32),
+                in_=w_scales[:, 0, 4 * q : 4 * q + 4, :].rearrange("e q n -> q e n").bitcast(I32),
+            )
+        chunks = [(0, 256, 256), (256, 256, 128), (512, 128, 32)]
+        x_rows = xT.rearrange("(p j) t -> p j t", j=PACK)
+        x_raw = []
+        for t0, width, cut in chunks:
+            raw = keep.tile([P, PACK, width], F32, name="x_raw%d" % t0)
+            nc.sync.dma_start(out=raw[:], in_=x_rows[:, :, t0 : t0 + width])
+            x_raw.append(raw)
+        nc.sync.dma_start(offsets[:], offs)
+        nc.sync.dma_start(out=bias[:], in_=b.rearrange("(a p t) e -> p a (t e)", p=P, t=PACK))
+        nc.sync.dma_start(out=gates[:], in_=gate[0:P, :])
+        nc.sync.dma_start(out=wp_raw[:], in_=wp.rearrange("(a p t) f -> p a t f", p=P, t=PACK))
+
+        def permute(dst, src, dt):
+            nc.vector.tensor_copy(
+                out=dst.bitcast(dt).rearrange("p (a t m) -> p a t m", t=PACK, m=P) if dt is U16 else dst.rearrange("p (a t m) -> p a t m", t=PACK, m=P),
+                in_=src.bitcast(dt).rearrange("p (a m t) -> p a t m", t=PACK, m=P) if dt is U16 else src.rearrange("p (a m t) -> p a t m", t=PACK, m=P),
+            )
+
+        for e in range(E):
+            permute(w_perm[:, e, :], w_raw[:, e, :], U16)
+        for e in range(E):
+            permute(s_perm[:, e, :], s_raw[:, e, :], U8)
+
+        for (t0, width, cut), raw in zip(chunks, x_raw):
+            grouped = keep.tile([P, width, PACK], BF16, align_bytes=64, name="x_bf%d" % t0)
+            view = raw[:].rearrange("p j t -> p t j")
+            nc.scalar.copy(out=grouped[:, 0:cut, :], in_=view[:, 0:cut, :])
+            if cut < width:
+                nc.vector.tensor_copy(out=grouped[:, cut:width, :], in_=view[:, cut:width, :])
+            nc.vector.quantize_mx(
+                out=codes[:, t0 : t0 + width].bitcast(FP8X4),
+                scales=scales[:, t0 : t0 + width],
+                in_=grouped[:].rearrange("p t j -> p (t j)"),
+            )
+
+        slot_codes = []
+        slot_scales = []
+        for e in range(E):
+            own = offsets[:, e * C // 16 : (e + 1) * C // 16]
+            sc = keep.tile([P, C], U32, align_bytes=64, name="slot_codes%d" % e)
+            ss = keep.tile([P, C], U8, align_bytes=64, name="slot_scales%d" % e)
+            nc.vector.tensor_copy(sc[:], codes[:].indirect(own))
+            nc.vector.tensor_copy(ss[:], scales[:].indirect(own))
+            slot_codes.append(sc)
+            slot_scales.append(ss)
+
+        hidden = {}
+        for e in range(E):
+            for a in range(PASSES):
+                h = keep.tile([P, PACK, C], F32, name="hidden%d%d" % (e, a))
+                hidden[e, a] = h
+                for half in range(2):
+                    bank = psum1.tile([P, 2, C], F32, name="bank")
+                    for i in range(2):
+                        t = 2 * half + i
+                        c0 = (a * PACK + t) * P
+                        nc.tensor.matmul_mx(
+                            out=bank[:, i, :],
+                            lhsT=w_perm[:, e, 2 * c0 : 2 * (c0 + P)].bitcast(FP4X4),
+                            lhsT_scale=s_perm[:, e, c0 : c0 + P],
+                            rhs=slot_codes[e][:].bitcast(FP8X4),
+                            rhs_scale=slot_scales[e][:],
+                            start=True,
+                            stop=True,
+                        )
+                        nc.scalar.activation(
+                            out=h[:, t, :], in_=bank[:, i, :], func=RELU, bias=bias[:, a, t * E + e : t * E + e + 1]
+                        )
+
+        for a in range(PASSES):
+            nc.scalar.copy(out=wp_bf[:, a], in_=wp_raw[:, a].rearrange("p t f -> p f t"))
+
+        def gated(e, a):
+            g = keep.tile([P, C, PACK], BF16, align_bytes=64, name="gated%d%d" % (e, a))
+            nc.vector.tensor_tensor(
+                out=g[:],
+                in0=hidden[e, a][:].rearrange("p t n -> p n t"),
+                in1=gates[:, e * C : (e + 1) * C].unsqueeze(2).to_broadcast([P, C, PACK]),
+                op=MULT,
+            )
+            return g
+
+        def quantised(e, a, g):
+            cq = keep.tile([P, C], U32, align_bytes=64, name="c_codes%d%d" % (e, a))
+            cs = keep.tile([P, C], U8, align_bytes=64, name="c_scales%d%d" % (e, a))
+            nc.vector.quantize_mx(out=cq[:].bitcast(FP8X4), scales=cs[:], in_=g[:].rearrange("p n t -> p (n t)"))
+            return cq, cs
+
+        def project(e, operands):
+            acc = psum2.tile([P, C], F32, name="acc")
+            for a in range(PASSES):
+                cq, cs = operands[a]
+                nc.tensor.matmul_mx(
+                    out=acc[:],
+                    lhsT=wp_codes[:, a * M : (a + 1) * M].bitcast(FP8X4),
+                    lhsT_scale=wp_scales[:, a * M : (a + 1) * M],
+                    rhs=cq[:].bitcast(FP8X4),
+                    rhs_scale=cs[:],
+                    start=(a == 0),
+                    stop=(a == PASSES - 1),
+                )
+            proj = keep.tile([P, C], F32, name="proj%d" % e)
+            nc.scalar.copy(out=proj[:], in_=acc[:])
+            return proj
+
+        def scatter(e, proj):
+            nc.vector.tensor_copy(result[:].indirect(offsets[:, e * C // 16 : (e + 1) * C // 16]), proj[:])
+
+        g00 = gated(0, 0)
+        g01 = gated(0, 1)
+        q00 = quantised(0, 0, g00)
+        nc.vector.quantize_mx(
+            out=wp_codes[:].bitcast(FP8X4), scales=wp_scales[:], in_=wp_bf[:].rearrange("p a f t -> p (a f t)")
+        )
+        q01 = quantised(0, 1, g01)
+        p0 = project(0, (q00, q01))
+        g10 = gated(1, 0)
+        g11 = gated(1, 1)
+        q10 = quantised(1, 0, g10)
+        q11 = quantised(1, 1, g11)
+        p1 = project(1, (q10, q11))
+        scatter(0, p0)
+        scatter(1, p1)
+        nc.sync.dma_start(out=out, in_=result[:])

@@ -19,6 +19,7 @@ U8 = mybir.dt.uint8
 FP8X4 = mybir.dt.float8_e4m3fn_x4
 FP4X4 = mybir.dt.float4_e2m1fn_x4
 RELU = mybir.ActivationFunctionType.Relu
+ADD = mybir.AluOpType.add
 MULT = mybir.AluOpType.mult
 
 
@@ -36,7 +37,7 @@ def tile_moe_nxt_lin_relu_kernel(tc, xT, w_words, w_scales, b, wp, gate, offs, o
         s_perm = keep.tile([P, E, N], U8, align_bytes=64, name="s_perm")
         codes = keep.tile([P, T], U32, align_bytes=64, name="codes")
         scales = keep.tile([P, T], U8, align_bytes=64, name="scales")
-        bias = keep.tile([P, PASSES, PACK * E], F32, name="bias")
+        bias = keep.tile([P, PASSES, PACK, E], F32, name="bias")
         gates = keep.tile([P, E * C], F32, name="gates")
         wp_raw = keep.tile([P, PASSES, PACK, M], F32, name="wp_raw")
         wp_bf = keep.tile([P, PASSES, M, PACK], BF16, align_bytes=64, name="wp_bf")
@@ -44,39 +45,48 @@ def tile_moe_nxt_lin_relu_kernel(tc, xT, w_words, w_scales, b, wp, gate, offs, o
         wp_scales = keep.tile([P, PASSES * M], U8, align_bytes=64, name="wp_scales")
         result = keep.tile([P, T], F32, name="result")
 
-        nc.vector.memset(s_raw[:].rearrange("p e n -> p (e n)").bitcast(I32), 0)
-        nc.gpsimd.memset(scales[:], 0)
-        nc.gpsimd.memset(result[:], 0.0)
+        nc.gpsimd.memset(s_raw[:].rearrange("p e n -> p (e n)").bitcast(I32), 0)
+        b_rows = b.rearrange("(a h t i) e -> a i h t e", a=PASSES, t=PACK, i=2)
+        wp_rows = wp.rearrange("(a h t i) f -> a i h t f", a=PASSES, t=PACK, i=2)
+        x_rows = xT.rearrange("(p j) t -> p j t", j=PACK)
+        chunks = [(0, 256, 96), (256, 256, 96), (512, 128, 48)]
+        x_raw = []
+        for t0, width, cut in chunks:
+            x_raw.append(keep.tile([P, PACK, width], F32, name="x_raw%d" % t0))
 
-        for e in range(E):
+        def load_words(e):
             nc.sync.dma_start(out=w_raw[:, e, :].bitcast(I32), in_=w_words[e, 0].bitcast(I32))
+
+        load_words(0)
         for q in range(4):
-            nc.scalar.dma_start(
+            nc.sync.dma_start(
                 out=s_raw[32 * q : 32 * q + 4, :, :].bitcast(I32),
                 in_=w_scales[:, 0, 4 * q : 4 * q + 4, :].rearrange("e q n -> q e n").bitcast(I32),
             )
-        chunks = [(0, 256, 256), (256, 256, 128), (512, 128, 32)]
-        x_rows = xT.rearrange("(p j) t -> p j t", j=PACK)
-        x_raw = []
-        for t0, width, cut in chunks:
-            raw = keep.tile([P, PACK, width], F32, name="x_raw%d" % t0)
+        for (t0, width, cut), raw in zip(chunks, x_raw):
             nc.sync.dma_start(out=raw[:], in_=x_rows[:, :, t0 : t0 + width])
-            x_raw.append(raw)
-        nc.sync.dma_start(offsets[:], offs)
-        nc.sync.dma_start(out=bias[:], in_=b.rearrange("(a p t) e -> p a (t e)", p=P, t=PACK))
+            if t0 == 0:
+                nc.sync.dma_start(offsets[:], offs)
+        for a in range(PASSES):
+            for i in range(2):
+                nc.sync.dma_start(out=bias[i:P:2, a, :, :], in_=b_rows[a, i])
+        for a in range(PASSES):
+            for i in range(2):
+                nc.sync.dma_start(out=wp_raw[i:P:2, a, :, :], in_=wp_rows[a, i])
+        load_words(1)
         nc.sync.dma_start(out=gates[:], in_=gate[0:P, :])
-        nc.sync.dma_start(out=wp_raw[:], in_=wp.rearrange("(a p t) f -> p a t f", p=P, t=PACK))
+        nc.gpsimd.memset(scales[:], 0)
+        nc.gpsimd.memset(result[:], 0.0)
 
-        def permute(dst, src, dt):
-            nc.vector.tensor_copy(
-                out=dst.bitcast(dt).rearrange("p (a t m) -> p a t m", t=PACK, m=P) if dt is U16 else dst.rearrange("p (a t m) -> p a t m", t=PACK, m=P),
-                in_=src.bitcast(dt).rearrange("p (a m t) -> p a t m", t=PACK, m=P) if dt is U16 else src.rearrange("p (a m t) -> p a t m", t=PACK, m=P),
+        def permute(engine, dst, src, dt):
+            engine.tensor_copy(
+                out=dst.bitcast(dt).rearrange("p (a t h) -> p a t h", a=PASSES, t=PACK),
+                in_=src.bitcast(dt).rearrange("p (a h t) -> p a t h", a=PASSES, t=PACK),
             )
 
+        permute(nc.vector, w_perm[:, 0, :], w_raw[:, 0, :], I32)
         for e in range(E):
-            permute(w_perm[:, e, :], w_raw[:, e, :], U16)
-        for e in range(E):
-            permute(s_perm[:, e, :], s_raw[:, e, :], U8)
+            permute(nc.vector, s_perm[:, e, :], s_raw[:, e, :], U16)
 
         for (t0, width, cut), raw in zip(chunks, x_raw):
             grouped = keep.tile([P, width, PACK], BF16, align_bytes=64, name="x_bf%d" % t0)
@@ -89,6 +99,12 @@ def tile_moe_nxt_lin_relu_kernel(tc, xT, w_words, w_scales, b, wp, gate, offs, o
                 scales=scales[:, t0 : t0 + width],
                 in_=grouped[:].rearrange("p t j -> p (t j)"),
             )
+
+        for a in range(PASSES):
+            nc.gpsimd.tensor_scalar(
+                out=wp_bf[:, a], in0=wp_raw[:, a].rearrange("p t f -> p f t"), scalar1=1.0, scalar2=0.0, op0=MULT, op1=ADD
+            )
+        permute(nc.gpsimd, w_perm[:, 1, :], w_raw[:, 1, :], I32)
 
         slot_codes = []
         slot_scales = []
@@ -120,12 +136,8 @@ def tile_moe_nxt_lin_relu_kernel(tc, xT, w_words, w_scales, b, wp, gate, offs, o
                             start=True,
                             stop=True,
                         )
-                        nc.scalar.activation(
-                            out=h[:, t, :], in_=bank[:, i, :], func=RELU, bias=bias[:, a, t * E + e : t * E + e + 1]
-                        )
-
-        for a in range(PASSES):
-            nc.scalar.copy(out=wp_bf[:, a], in_=wp_raw[:, a].rearrange("p t f -> p f t"))
+                        own_bias = bias[:, a, t, e : e + 1]
+                        nc.scalar.activation(out=h[:, t, :], in_=bank[:, i, :], func=RELU, bias=own_bias)
 
         def gated(e, a):
             g = keep.tile([P, C, PACK], BF16, align_bytes=64, name="gated%d%d" % (e, a))
@@ -165,10 +177,10 @@ def tile_moe_nxt_lin_relu_kernel(tc, xT, w_words, w_scales, b, wp, gate, offs, o
 
         g00 = gated(0, 0)
         g01 = gated(0, 1)
-        q00 = quantised(0, 0, g00)
         nc.vector.quantize_mx(
             out=wp_codes[:].bitcast(FP8X4), scales=wp_scales[:], in_=wp_bf[:].rearrange("p a f t -> p (a f t)")
         )
+        q00 = quantised(0, 0, g00)
         q01 = quantised(0, 1, g01)
         p0 = project(0, (q00, q01))
         g10 = gated(1, 0)

@@ -45,8 +45,13 @@ def tile_moe_nxt_lin_relu_kernel(tc, xT, w_words, w_scales, b, wp, gate, offs, o
         wp_scales = keep.tile([P, PASSES * M], U8, align_bytes=64, name="wp_scales")
         result = keep.tile([P, T], F32, name="result")
 
-        nc.gpsimd.memset(s_raw[:].rearrange("p e n -> p (e n)").bitcast(I32), 0)
+        nc.vector.memset(s_raw[:].rearrange("p e n -> p (e n)").bitcast(I32), 0)
+        nc.vector.memset(scales[:].bitcast(I32), 0)
+        nc.vector.memset(result[:], 0.0)
         b_rows = b.rearrange("(a h t i) e -> a i h t e", a=PASSES, t=PACK, i=2)
+        for a in range(PASSES):
+            for i in range(2):
+                nc.gpsimd.dma_start(out=bias[i:P:2, a, :, :], in_=b_rows[a, i])
         wp_rows = wp.rearrange("(a h t i) f -> a i h t f", a=PASSES, t=PACK, i=2)
         x_rows = xT.rearrange("(p j) t -> p j t", j=PACK)
         chunks = [(0, 256, 96), (256, 256, 96), (512, 128, 48)]
@@ -69,14 +74,9 @@ def tile_moe_nxt_lin_relu_kernel(tc, xT, w_words, w_scales, b, wp, gate, offs, o
                 nc.sync.dma_start(offsets[:], offs)
         for a in range(PASSES):
             for i in range(2):
-                nc.sync.dma_start(out=bias[i:P:2, a, :, :], in_=b_rows[a, i])
-        for a in range(PASSES):
-            for i in range(2):
                 nc.sync.dma_start(out=wp_raw[i:P:2, a, :, :], in_=wp_rows[a, i])
         load_words(1)
         nc.sync.dma_start(out=gates[:], in_=gate[0:P, :])
-        nc.gpsimd.memset(scales[:], 0)
-        nc.gpsimd.memset(result[:], 0.0)
 
         def permute(engine, dst, src, dt):
             engine.tensor_copy(
@@ -88,12 +88,16 @@ def tile_moe_nxt_lin_relu_kernel(tc, xT, w_words, w_scales, b, wp, gate, offs, o
         for e in range(E):
             permute(nc.vector, s_perm[:, e, :], s_raw[:, e, :], U16)
 
+        def four(x):
+            return x.rearrange("p (c i) t -> p c t i", i=4)
+
+        def four_in(x):
+            return x.rearrange("p t (c i) -> p c t i", i=4)
+
         for (t0, width, cut), raw in zip(chunks, x_raw):
             grouped = keep.tile([P, width, PACK], BF16, align_bytes=64, name="x_bf%d" % t0)
-            view = raw[:].rearrange("p j t -> p t j")
-            nc.scalar.copy(out=grouped[:, 0:cut, :], in_=view[:, 0:cut, :])
-            if cut < width:
-                nc.vector.tensor_copy(out=grouped[:, cut:width, :], in_=view[:, cut:width, :])
+            nc.scalar.copy(out=four(grouped[:, 0:cut, :]), in_=four_in(raw[:, :, 0:cut]))
+            nc.vector.tensor_copy(out=four(grouped[:, cut:width, :]), in_=four_in(raw[:, :, cut:width]))
             nc.vector.quantize_mx(
                 out=codes[:, t0 : t0 + width].bitcast(FP8X4),
                 scales=scales[:, t0 : t0 + width],
@@ -102,7 +106,7 @@ def tile_moe_nxt_lin_relu_kernel(tc, xT, w_words, w_scales, b, wp, gate, offs, o
 
         for a in range(PASSES):
             nc.gpsimd.tensor_scalar(
-                out=wp_bf[:, a], in0=wp_raw[:, a].rearrange("p t f -> p f t"), scalar1=1.0, scalar2=0.0, op0=MULT, op1=ADD
+                out=four(wp_bf[:, a]), in0=four_in(wp_raw[:, a]), scalar1=1.0, scalar2=0.0, op0=MULT, op1=ADD
             )
         permute(nc.gpsimd, w_perm[:, 1, :], w_raw[:, 1, :], I32)
 
@@ -142,9 +146,9 @@ def tile_moe_nxt_lin_relu_kernel(tc, xT, w_words, w_scales, b, wp, gate, offs, o
         def gated(e, a):
             g = keep.tile([P, C, PACK], BF16, align_bytes=64, name="gated%d%d" % (e, a))
             nc.vector.tensor_tensor(
-                out=g[:],
-                in0=hidden[e, a][:].rearrange("p t n -> p n t"),
-                in1=gates[:, e * C : (e + 1) * C].unsqueeze(2).to_broadcast([P, C, PACK]),
+                out=four(g[:]),
+                in0=four_in(hidden[e, a][:]),
+                in1=gates[:, e * C : (e + 1) * C].rearrange("p (c i) -> p c i", i=4).unsqueeze(2).to_broadcast([P, C // 4, PACK, 4]),
                 op=MULT,
             )
             return g

@@ -70,8 +70,7 @@ def tile_moe_nxt_lin_relu_kernel(tc, xT, w_words, w_scales, b, wp, gate, offs, o
             )
         for (t0, width, cut), raw in zip(chunks, x_raw):
             nc.sync.dma_start(out=raw[:], in_=x_rows[:, :, t0 : t0 + width])
-            if t0 == 0:
-                nc.sync.dma_start(offsets[:], offs)
+        nc.sync.dma_start(offsets[:], offs)
         for a in range(PASSES):
             for i in range(2):
                 nc.sync.dma_start(out=wp_raw[i:P:2, a, :, :], in_=wp_rows[a, i])
@@ -108,7 +107,6 @@ def tile_moe_nxt_lin_relu_kernel(tc, xT, w_words, w_scales, b, wp, gate, offs, o
             nc.gpsimd.tensor_scalar(
                 out=four(wp_bf[:, a]), in0=four_in(wp_raw[:, a]), scalar1=1.0, scalar2=0.0, op0=MULT, op1=ADD
             )
-        permute(nc.gpsimd, w_perm[:, 1, :], w_raw[:, 1, :], I32)
 
         slot_codes = []
         slot_scales = []
@@ -120,6 +118,8 @@ def tile_moe_nxt_lin_relu_kernel(tc, xT, w_words, w_scales, b, wp, gate, offs, o
             nc.vector.tensor_copy(ss[:], scales[:].indirect(own))
             slot_codes.append(sc)
             slot_scales.append(ss)
+
+        permute(nc.vector, w_perm[:, 1, :], w_raw[:, 1, :], I32)
 
         hidden = {}
         for e in range(E):

from contextlib import ExitStack

import concourse.mybir as mybir

K, T, E, C, N, M = 512, 640, 2, 256, 1024, 128
P = 128
PACK = 4
PASSES = N // 512

FLOPS = 2 * E * C * K * N + 2 * E * C * N * M
BYTES = 4 * K * T + E * K * N // 2 + E * K * N // 32 + 4 * N * E + 4 * N * M + 4 * E * C + 2 * P * (E * C // 16) + 4 * M * T

F32 = mybir.dt.float32
BF16 = mybir.dt.bfloat16
I32 = mybir.dt.int32
U32 = mybir.dt.uint32
U16 = mybir.dt.uint16
U8 = mybir.dt.uint8
FP8X4 = mybir.dt.float8_e4m3fn_x4
FP4X4 = mybir.dt.float4_e2m1fn_x4
RELU = mybir.ActivationFunctionType.Relu
ADD = mybir.AluOpType.add
MULT = mybir.AluOpType.mult


def tile_moe_nxt_lin_relu_kernel(tc, xT, w_words, w_scales, b, wp, gate, offs, out):
    nc = tc.nc
    with ExitStack() as ctx:
        keep = ctx.enter_context(tc.tile_pool(name="keep", bufs=1))
        psum1 = ctx.enter_context(tc.psum_pool(name="psum1", bufs=6))
        psum2 = ctx.enter_context(tc.psum_pool(name="psum2", bufs=2))

        offsets = keep.tile([P, E * C // 16], U16, name="offsets")
        w_raw = keep.tile([P, E, 2 * N], U8, align_bytes=64, name="w_raw")
        w_perm = keep.tile([P, E, 2 * N], U8, align_bytes=64, name="w_perm")
        s_raw = keep.tile([P, E, N], U8, align_bytes=64, name="s_raw")
        s_perm = keep.tile([P, E, N], U8, align_bytes=64, name="s_perm")
        codes = keep.tile([P, T], U32, align_bytes=64, name="codes")
        scales = keep.tile([P, T], U8, align_bytes=64, name="scales")
        bias = keep.tile([P, PASSES, PACK, E], F32, name="bias")
        gates = keep.tile([P, E * C], F32, name="gates")
        wp_raw = keep.tile([P, PASSES, PACK, M], F32, name="wp_raw")
        wp_bf = keep.tile([P, PASSES, M, PACK], BF16, align_bytes=64, name="wp_bf")
        wp_codes = keep.tile([P, PASSES * M], U32, align_bytes=64, name="wp_codes")
        wp_scales = keep.tile([P, PASSES * M], U8, align_bytes=64, name="wp_scales")
        result = keep.tile([P, T], F32, name="result")

        nc.vector.memset(s_raw[:].rearrange("p e n -> p (e n)").bitcast(I32), 0)
        nc.vector.memset(scales[:].bitcast(I32), 0)
        nc.vector.memset(result[:], 0.0)
        b_rows = b.rearrange("(a h t i) e -> a i h t e", a=PASSES, t=PACK, i=2)
        for a in range(PASSES):
            for i in range(2):
                nc.gpsimd.dma_start(out=bias[i:P:2, a, :, :], in_=b_rows[a, i])
        wp_rows = wp.rearrange("(a h t i) f -> a i h t f", a=PASSES, t=PACK, i=2)
        x_rows = xT.rearrange("(p j) t -> p j t", j=PACK)
        chunks = [(0, 256, 96), (256, 256, 96), (512, 128, 48)]
        x_raw = []
        for t0, width, cut in chunks:
            x_raw.append(keep.tile([P, PACK, width], F32, name="x_raw%d" % t0))

        def load_words(e):
            nc.sync.dma_start(out=w_raw[:, e, :].bitcast(I32), in_=w_words[e, 0].bitcast(I32))

        load_words(0)
        for q in range(4):
            nc.sync.dma_start(
                out=s_raw[32 * q : 32 * q + 4, :, :].bitcast(I32),
                in_=w_scales[:, 0, 4 * q : 4 * q + 4, :].rearrange("e q n -> q e n").bitcast(I32),
            )
        for (t0, width, cut), raw in zip(chunks, x_raw):
            nc.sync.dma_start(out=raw[:], in_=x_rows[:, :, t0 : t0 + width])
        nc.sync.dma_start(offsets[:], offs)
        for a in range(PASSES):
            for i in range(2):
                nc.sync.dma_start(out=wp_raw[i:P:2, a, :, :], in_=wp_rows[a, i])
        load_words(1)
        nc.sync.dma_start(out=gates[:], in_=gate[0:P, :])

        def permute(engine, dst, src, dt):
            engine.tensor_copy(
                out=dst.bitcast(dt).rearrange("p (a t h) -> p a t h", a=PASSES, t=PACK),
                in_=src.bitcast(dt).rearrange("p (a h t) -> p a t h", a=PASSES, t=PACK),
            )

        permute(nc.vector, w_perm[:, 0, :], w_raw[:, 0, :], I32)
        for e in range(E):
            permute(nc.vector, s_perm[:, e, :], s_raw[:, e, :], U16)

        def four(x):
            return x.rearrange("p (c i) t -> p c t i", i=4)

        def four_in(x):
            return x.rearrange("p t (c i) -> p c t i", i=4)

        for (t0, width, cut), raw in zip(chunks, x_raw):
            grouped = keep.tile([P, width, PACK], BF16, align_bytes=64, name="x_bf%d" % t0)
            nc.scalar.copy(out=four(grouped[:, 0:cut, :]), in_=four_in(raw[:, :, 0:cut]))
            nc.vector.tensor_copy(out=four(grouped[:, cut:width, :]), in_=four_in(raw[:, :, cut:width]))
            nc.vector.quantize_mx(
                out=codes[:, t0 : t0 + width].bitcast(FP8X4),
                scales=scales[:, t0 : t0 + width],
                in_=grouped[:].rearrange("p t j -> p (t j)"),
            )

        for a in range(PASSES):
            nc.gpsimd.tensor_scalar(
                out=four(wp_bf[:, a]), in0=four_in(wp_raw[:, a]), scalar1=1.0, scalar2=0.0, op0=MULT, op1=ADD
            )

        slot_codes = []
        slot_scales = []
        for e in range(E):
            own = offsets[:, e * C // 16 : (e + 1) * C // 16]
            sc = keep.tile([P, C], U32, align_bytes=64, name="slot_codes%d" % e)
            ss = keep.tile([P, C], U8, align_bytes=64, name="slot_scales%d" % e)
            nc.vector.tensor_copy(sc[:], codes[:].indirect(own))
            nc.vector.tensor_copy(ss[:], scales[:].indirect(own))
            slot_codes.append(sc)
            slot_scales.append(ss)

        permute(nc.vector, w_perm[:, 1, :], w_raw[:, 1, :], I32)

        hidden = {}
        for e in range(E):
            for a in range(PASSES):
                h = keep.tile([P, PACK, C], F32, name="hidden%d%d" % (e, a))
                hidden[e, a] = h
                for half in range(2):
                    bank = psum1.tile([P, 2, C], F32, name="bank")
                    for i in range(2):
                        t = 2 * half + i
                        c0 = (a * PACK + t) * P
                        nc.tensor.matmul_mx(
                            out=bank[:, i, :],
                            lhsT=w_perm[:, e, 2 * c0 : 2 * (c0 + P)].bitcast(FP4X4),
                            lhsT_scale=s_perm[:, e, c0 : c0 + P],
                            rhs=slot_codes[e][:].bitcast(FP8X4),
                            rhs_scale=slot_scales[e][:],
                            start=True,
                            stop=True,
                        )
                        own_bias = bias[:, a, t, e : e + 1]
                        nc.scalar.activation(out=h[:, t, :], in_=bank[:, i, :], func=RELU, bias=own_bias)

        def gated(e, a):
            g = keep.tile([P, C, PACK], BF16, align_bytes=64, name="gated%d%d" % (e, a))
            nc.vector.tensor_tensor(
                out=four(g[:]),
                in0=four_in(hidden[e, a][:]),
                in1=gates[:, e * C : (e + 1) * C].rearrange("p (c i) -> p c i", i=4).unsqueeze(2).to_broadcast([P, C // 4, PACK, 4]),
                op=MULT,
            )
            return g

        def quantised(e, a, g):
            cq = keep.tile([P, C], U32, align_bytes=64, name="c_codes%d%d" % (e, a))
            cs = keep.tile([P, C], U8, align_bytes=64, name="c_scales%d%d" % (e, a))
            nc.vector.quantize_mx(out=cq[:].bitcast(FP8X4), scales=cs[:], in_=g[:].rearrange("p n t -> p (n t)"))
            return cq, cs

        def project(e, operands):
            acc = psum2.tile([P, C], F32, name="acc")
            for a in range(PASSES):
                cq, cs = operands[a]
                nc.tensor.matmul_mx(
                    out=acc[:],
                    lhsT=wp_codes[:, a * M : (a + 1) * M].bitcast(FP8X4),
                    lhsT_scale=wp_scales[:, a * M : (a + 1) * M],
                    rhs=cq[:].bitcast(FP8X4),
                    rhs_scale=cs[:],
                    start=(a == 0),
                    stop=(a == PASSES - 1),
                )
            proj = keep.tile([P, C], F32, name="proj%d" % e)
            nc.scalar.copy(out=proj[:], in_=acc[:])
            return proj

        def scatter(e, proj):
            nc.vector.tensor_copy(result[:].indirect(offsets[:, e * C // 16 : (e + 1) * C // 16]), proj[:])

        g00 = gated(0, 0)
        g01 = gated(0, 1)
        nc.vector.quantize_mx(
            out=wp_codes[:].bitcast(FP8X4), scales=wp_scales[:], in_=wp_bf[:].rearrange("p a f t -> p (a f t)")
        )
        q00 = quantised(0, 0, g00)
        q01 = quantised(0, 1, g01)
        p0 = project(0, (q00, q01))
        g10 = gated(1, 0)
        g11 = gated(1, 1)
        q10 = quantised(1, 0, g10)
        q11 = quantised(1, 1, g11)
        p1 = project(1, (q10, q11))
        scatter(0, p0)
        scatter(1, p1)
        nc.sync.dma_start(out=out, in_=result[:])
